import numpy as np
import ml_dtypes


def mxq(x, axis, fmt="e4m3"):
    dtype, down = {"e4m3": (ml_dtypes.float8_e4m3fn, 7), "e5m2": (ml_dtypes.float8_e5m2, 14)}[fmt]
    v = np.moveaxis(np.asarray(x, np.float32).astype(ml_dtypes.bfloat16).astype(np.float64), axis, -1)
    blocks = v.reshape(v.shape[:-1] + (-1, 32))
    amax = np.abs(blocks).max(-1, keepdims=True)
    byte = np.maximum(np.where(amax > 0, np.frexp(amax)[1] - 1 + 127, 0) - down, 1)
    scale = np.exp2(byte - 127.0)
    codes = (blocks / scale).astype(np.float32).astype(dtype).astype(np.float64)
    return np.moveaxis((codes * scale).reshape(v.shape), -1, axis)


WIDE = False


def mx_kscale(k):
    if not WIDE:
        return np.ones(k)
    levels = np.array([10, -10, 5, -5, 0])
    if k % 512:
        return np.exp2(np.random.permutation(np.resize(levels, k // 32))).repeat(32)
    a = np.empty((k // 512, 16))
    for p in range(k // 512):
        a[p, :8] = np.random.permutation(np.resize(levels, 8))
        for g in range(8):
            far = levels[np.abs(levels - a[p, g]) >= 10]
            a[p, g + 8] = far[np.random.randint(len(far))]
    return np.exp2(a.ravel()).repeat(32)


def f64(x):
    return np.asarray(x).astype(np.float64)


E2M1 = np.array([0.0, 0.5, 1.0, 1.5, 2.0, 3.0, 4.0, 6.0, -0.0, -0.5, -1.0, -1.5, -2.0, -3.0, -4.0, -6.0])


def pack_weight(w, fmt):
    k, n = w.shape
    w = f64(np.asarray(w, np.float32).astype(ml_dtypes.bfloat16)).reshape(k // 32, 32, n)
    amax = np.abs(w).max(1)
    if fmt == "e4m3":
        byte = np.frexp(amax)[1] - 1 + 127 - 7
    else:
        mant, ex = np.frexp(amax / 6.0)
        byte = np.where(mant > 0.5, ex, ex - 1) + 127
    byte = np.clip(np.where(amax > 0, byte, 1), 1, 254)
    scaled = (w * np.exp2(127.0 - byte)[:, None, :]).reshape(k, n).astype(np.float32)
    by_word = np.ascontiguousarray(scaled.reshape(k // 512, 128, 4, n).transpose(0, 1, 3, 2))
    if fmt == "e4m3":
        words = by_word.astype(ml_dtypes.float8_e4m3fn).view(np.uint8)
    else:
        c = by_word.astype(ml_dtypes.float4_e2m1fn).view(np.uint8) & 0xF
        words = (c[..., 0::2] | (c[..., 1::2] << 4)).reshape(k // 512, 128, 2 * n)
    return np.ascontiguousarray(words), np.ascontiguousarray(byte.astype(np.uint8).reshape(k // 512, 16, n))


def unpack_weight(words, scales, fmt):
    g, _, n = scales.shape
    words = np.ascontiguousarray(words).reshape(g, 128, n, -1)
    if fmt == "e4m3":
        vals = words.view(ml_dtypes.float8_e4m3fn).astype(np.float64)
    else:
        nib = np.empty((g, 128, n, 4), np.uint8)
        nib[..., 0::2] = words & 0xF
        nib[..., 1::2] = words >> 4
        vals = E2M1[nib]
    vals = vals * np.repeat(np.exp2(scales.astype(np.float64) - 127.0), 8, axis=1)[..., None]
    return vals.transpose(0, 1, 3, 2).reshape(g * 512, n)


def sigmoid(v):
    return 1.0 / (1.0 + np.exp(-v))


K, L, T, B, N = 1024, 512, 1024, 128, 512


def setup_inputs():
    n = np.random.standard_normal
    fk = mx_kscale(K)
    fl = mx_kscale(L)
    xtp = pack_weight(n((K, T)) / fk[:, None], "e4m3")
    wvp = pack_weight(n((K, N)) * 1 / np.sqrt(K) * fk[:, None], "e2m1")
    wqp = pack_weight(n((L, N)) * 1 / np.sqrt(L) * fl[:, None], "e2m1")
    wgp = pack_weight(n((K, N)) * 1 / np.sqrt(K) * fk[:, None], "e4m3")
    return {
        "xt_words": xtp[0],
        "xt_scales": xtp[1],
        "wv_words": wvp[0],
        "wv_scales": wvp[1],
        "xq": (n((L, T)) / fl[:, None]).astype(np.float32),
        "wq_words": wqp[0],
        "wq_scales": wqp[1],
        "wg_words": wgp[0],
        "wg_scales": wgp[1],
        "bw": (np.random.uniform(0.5, 2.0, (1, B))).astype(np.float32),
    }


def reference(xt_words, xt_scales, wv_words, wv_scales, xq, wq_words, wq_scales, wg_words, wg_scales, bw):
    xtu = unpack_weight(xt_words, xt_scales, "e4m3")
    wvu = unpack_weight(wv_words, wv_scales, "e2m1")
    wqu = unpack_weight(wq_words, wq_scales, "e2m1")
    wgu = unpack_weight(wg_words, wg_scales, "e4m3")
    xqq = mxq(f64(xq), 0, "e4m3")
    v = wvu.T @ xtu + wqu.T @ xqq
    g = wgu.T @ xtu
    s = sigmoid(g)
    num = (s * v).reshape(N, B, T // B).sum(axis=2)
    den = s.reshape(N, B, T // B).sum(axis=2)
    y = f64(bw) * num / (den + 0.1)
    return y

@@ -1,0 +1,271 @@
+from contextlib import ExitStack
+
+import concourse.mybir as mybir
+
+K, L, T, B, N = 1024, 512, 1024, 128, 512
+FLOPS = 2 * N * T * (2 * K + L)
+
+F32 = mybir.dt.float32
+BF16 = mybir.dt.bfloat16
+I32 = mybir.dt.int32
+U32 = mybir.dt.uint32
+U8 = mybir.dt.uint8
+FP8X4 = mybir.dt.float8_e4m3fn_x4
+FP4X4 = mybir.dt.float4_e2m1fn_x4
+ACT = mybir.ActivationFunctionType
+ALU = mybir.AluOpType
+AX = mybir.AxisListType
+
+P = 128
+PACK = 4
+PASSES = K // (P * PACK)
+HALF = 512
+HALVES = T // HALF
+CHUNK = 256
+TILES = N // P
+GROUP = T // B
+GROUPS = HALF // GROUP
+WG_ROW = 4
+
+
+def tile_mix_gated_mean_of_neighbours_kernel(
+    tc, xt_words, xt_scales, wv_words, wv_scales, xq, wq_words, wq_scales, wg_words, wg_scales, bw, out
+):
+    nc = tc.nc
+
+    with ExitStack() as ctx:
+        keep = ctx.enter_context(tc.tile_pool(name="keep", bufs=1))
+        psum = ctx.enter_context(tc.psum_pool(name="psum", bufs=8))
+        ctx.enter_context(tc.manual_schedule())
+
+        def sb(name, shape, dtype):
+            return keep.tile(shape, dtype, name=name, align_bytes=64)
+
+        plane_x = sb("plane_x", [P, PASSES * T], U8)
+        plane_v = sb("plane_v", [P, PASSES * N], U8)
+        plane_q = sb("plane_q", [P, N], U8)
+        wg = sb("wg", [P, PASSES, N], U32)
+        wv = sb("wv", [P, PASSES, 2 * N], U8)
+        wq = sb("wq", [P, 2 * N], U8)
+        xt = [sb("xt%d" % h, [P, PASSES, HALF], U32) for h in range(HALVES)]
+        xq_raw = [sb("xq_raw%d" % c, [P, PACK, CHUNK], F32) for c in range(T // CHUNK)]
+        xq_bf = [sb("xq_bf%d" % c, [P, CHUNK * PACK], BF16) for c in range(T // CHUNK)]
+        xq_codes = [sb("xq_codes%d" % h, [P, HALF], U32) for h in range(HALVES)]
+        xq_plane = [sb("xq_plane%d" % h, [P, HALF], U8) for h in range(HALVES)]
+        bw_all = sb("bw_all", [P, B], F32)
+        warm = sb("warm", [P, 2], F32)
+        gate = {(h, i): sb("gate%d%d" % (h, i), [P, HALF], F32) for h in range(HALVES) for i in range(TILES)}
+        prod = {(h, i): sb("prod%d%d" % (h, i), [P, HALF], F32) for h in range(HALVES) for i in range(TILES)}
+        fold = {(h, i): sb("fold%d%d" % (h, i), [P, GROUPS, 4], F32) for h in range(HALVES) for i in range(TILES)}
+        den = [sb("den%d" % h, [P, TILES, GROUPS], F32) for h in range(HALVES)]
+        den4 = sb("den4", [P, TILES, GROUPS, 4], F32)
+        den2 = sb("den2", [P, TILES * GROUPS, 2], F32)
+        root = sb("root", [P, TILES, B], F32)
+        recip = sb("recip", [P, TILES, B], F32)
+        factor = [sb("factor%d" % u, [P, 2, B], F32) for u in range(2)]
+        num = [sb("num%d" % i, [P, B], F32) for i in range(TILES)]
+        res = [sb("res%d" % i, [P, B], F32) for i in range(TILES)]
+
+        def load_scales(queue, plane, row, scales, quad):
+            passes, width = scales.shape[0], scales.shape[2]
+            dst = plane[32 * quad + row : 32 * quad + row + 4, 0 : passes * width].bitcast(I32)
+            src = scales[:, 4 * quad : 4 * quad + 4, :].bitcast(I32)
+            queue.dma_start(out=dst.rearrange("r (z c) -> r z c", z=passes), in_=src.rearrange("z r c -> r z c"))
+
+        def load_xt(h):
+            src = xt_words.rearrange("z p c r -> p z (c r)")[:, :, PACK * HALF * h : PACK * HALF * (h + 1)]
+            nc.sync.dma_start(out=xt[h][:].bitcast(I32), in_=src.bitcast(I32))
+
+        def load_xq(c):
+            src = xq[:, CHUNK * c : CHUNK * (c + 1)].rearrange("(p j) t -> p j t", j=PACK)
+            nc.sync.dma_start(out=xq_raw[c][:], in_=src)
+
+        nc.vector.memset(plane_x[:].bitcast(I32), 0)
+        nc.vector.memset(warm[:, 0:1], 0.0)
+        nc.gpsimd.memset(plane_v[:].bitcast(I32), 0)
+        nc.gpsimd.memset(plane_q[:].bitcast(I32), 0)
+        nc.scalar.activation(out=warm[:, 1:2], in_=warm[:, 0:1], func=ACT.Sigmoid)
+
+        nc.sync.dma_start(out=wg[:].bitcast(I32), in_=wg_words.rearrange("z p c r -> p z (c r)").bitcast(I32))
+        for quad in range(4):
+            load_scales(nc.sync, plane_x, 0, xt_scales, quad)
+        for quad in range(2):
+            load_scales(nc.sync, plane_x, WG_ROW, wg_scales, quad)
+        load_xt(0)
+        for quad in range(2, 4):
+            load_scales(nc.sync, plane_x, WG_ROW, wg_scales, quad)
+        for quad in range(4):
+            load_scales(nc.gpsimd, plane_v, 0, wv_scales, quad)
+        load_xt(1)
+        load_xq(0)
+        load_xq(1)
+        nc.sync.dma_start(out=wv[:].bitcast(I32), in_=wv_words.rearrange("z p c -> p z c").bitcast(I32))
+        nc.sync.dma_start(out=wq[:].bitcast(I32), in_=wq_words[0].bitcast(I32))
+        for quad in range(4):
+            load_scales(nc.sync, plane_q, 0, wq_scales, quad)
+        load_xq(2)
+        load_xq(3)
+        nc.sync.dma_start(out=bw_all[:], in_=bw[0].partition_broadcast(P))
+
+        def xt_plane(h, z):
+            return plane_x[:, T * z + HALF * h : T * z + HALF * (h + 1)]
+
+        def gates(h, i):
+            acc = psum.tile([P, HALF], F32, name="acc")
+            for z in range(PASSES):
+                nc.tensor.matmul_mx(
+                    out=acc[:],
+                    lhsT=wg[:, z, P * i : P * (i + 1)].bitcast(FP8X4),
+                    lhsT_scale=plane_x[WG_ROW:P, N * z + P * i : N * z + P * (i + 1)],
+                    rhs=xt[h][:, z, :].bitcast(FP8X4),
+                    rhs_scale=xt_plane(h, z),
+                    start=(z == 0),
+                    stop=(z == PASSES - 1),
+                )
+            nc.scalar.activation(out=gate[h, i][:], in_=acc[:], func=ACT.Sigmoid)
+
+        value = {}
+
+        def values(h, i):
+            acc = psum.tile([P, HALF], F32, name="acc")
+            for z in range(PASSES):
+                nc.tensor.matmul_mx(
+                    out=acc[:],
+                    lhsT=wv[:, z, 2 * P * i : 2 * P * (i + 1)].bitcast(FP4X4),
+                    lhsT_scale=plane_v[:, N * z + P * i : N * z + P * (i + 1)],
+                    rhs=xt[h][:, z, :].bitcast(FP8X4),
+                    rhs_scale=xt_plane(h, z),
+                    start=(z == 0),
+                    stop=False,
+                )
+            nc.tensor.matmul_mx(
+                out=acc[:],
+                lhsT=wq[:, 2 * P * i : 2 * P * (i + 1)].bitcast(FP4X4),
+                lhsT_scale=plane_q[:, P * i : P * (i + 1)],
+                rhs=xq_codes[h][:].bitcast(FP8X4),
+                rhs_scale=xq_plane[h][:],
+                start=False,
+                stop=True,
+            )
+            value[h, i] = acc
+
+        def cast_views(c):
+            dst = xq_bf[c][:].rearrange("p (c i j) -> p c j i", i=4, j=PACK)
+            src = xq_raw[c][:].rearrange("p j (c i) -> p c j i", i=4)
+            return dst, src
+
+        def quantise(c):
+            h, u = divmod(c, HALF // CHUNK)
+            cols = slice(CHUNK * u, CHUNK * (u + 1))
+            nc.vector.quantize_mx(
+                out=xq_codes[h][:, cols].bitcast(FP8X4), scales=xq_plane[h][:, cols], in_=xq_bf[c][:]
+            )
+
+        def by_group(t):
+            return t[:].rearrange("p (b j) -> p b j", j=GROUP)
+
+        def den_on_vector(h, i):
+            nc.vector.tensor_reduce(out=den[h][:, i, :], in_=by_group(gate[h, i]), axis=AX.X, op=ALU.add)
+
+        def fold_halves(dst, t):
+            g = by_group(t)
+            nc.gpsimd.tensor_tensor(out=dst, in0=g[:, :, 0:4], in1=g[:, :, 4:8], op=ALU.add)
+
+        def product(h, i):
+            nc.vector.tensor_tensor(out=prod[h, i][:], in0=value[h, i][:], in1=gate[h, i][:], op=ALU.mult)
+
+        def num_cols(h, i):
+            return num[i][:, GROUPS * h : GROUPS * (h + 1)]
+
+        def num_whole(h, i):
+            nc.vector.tensor_reduce(out=num_cols(h, i), in_=by_group(prod[h, i]), axis=AX.X, op=ALU.add)
+
+        def num_fold(h, i):
+            fold_halves(fold[h, i][:], prod[h, i])
+
+        def num_folded(h, i):
+            nc.vector.tensor_reduce(out=num_cols(h, i), in_=fold[h, i][:], axis=AX.X, op=ALU.add)
+
+        def weigh(u):
+            nc.gpsimd.tensor_tensor(
+                out=factor[u][:],
+                in0=recip[:, 2 * u : 2 * u + 2, :],
+                in1=bw_all[:].unsqueeze(1).to_broadcast([P, 2, B]),
+                op=ALU.mult,
+            )
+
+        def finish(engine, i):
+            engine.tensor_tensor(out=res[i][:], in0=num[i][:], in1=factor[i // 2][:, i % 2, :], op=ALU.mult)
+            nc.sync.dma_start(out=out[P * i : P * (i + 1), :], in_=res[i][:])
+
+        for i in range(TILES):
+            gates(0, i)
+            den_on_vector(0, i)
+        for i in range(TILES):
+            gates(1, i)
+
+        nc.gpsimd.tensor_scalar(
+            out=xq_bf[0][:].rearrange("p (t j) -> p t j", j=PACK),
+            in0=xq_raw[0][:].rearrange("p j t -> p t j"),
+            scalar1=1.0,
+            scalar2=0.0,
+            op0=ALU.mult,
+            op1=ALU.add,
+        )
+        dst, src = cast_views(1)
+        nc.vector.tensor_copy(out=dst, in_=src)
+        quantise(0)
+        quantise(1)
+        for c in (2, 3):
+            dst, src = cast_views(c)
+            nc.scalar.copy(out=dst, in_=src)
+
+        for i in range(TILES):
+            fold_halves(den4[:, i, :, :], gate[1, i])
+        quarters = den4[:].rearrange("p i b j -> p (i b) j")
+        nc.gpsimd.tensor_tensor(out=den2[:], in0=quarters[:, :, 0:2], in1=quarters[:, :, 2:4], op=ALU.add)
+        nc.gpsimd.tensor_tensor(
+            out=den[1][:].rearrange("p i b -> p (i b)"), in0=den2[:, :, 0], in1=den2[:, :, 1], op=ALU.add
+        )
+        for h in range(HALVES):
+            nc.scalar.activation(
+                out=root[:, :, GROUPS * h : GROUPS * (h + 1)], in_=den[h][:], func=ACT.Abs_reciprocal_sqrt, bias=0.1
+            )
+        nc.scalar.activation(out=recip[:], in_=root[:], func=ACT.Square)
+
+        values(0, 0)
+        product(0, 0)
+        num_whole(0, 0)
+        values(0, 1)
+        product(0, 1)
+        values(0, 2)
+        product(0, 2)
+        quantise(2)
+        quantise(3)
+        num_whole(0, 1)
+        num_whole(0, 2)
+        values(0, 3)
+        product(0, 3)
+        num_fold(0, 3)
+        values(1, 0)
+        product(1, 0)
+        num_fold(1, 0)
+        num_folded(0, 3)
+        weigh(0)
+        values(1, 1)
+        product(1, 1)
+        num_fold(1, 1)
+        num_folded(1, 0)
+        weigh(1)
+        values(1, 2)
+        product(1, 2)
+        num_fold(1, 2)
+        num_folded(1, 1)
+        values(1, 3)
+        product(1, 3)
+        num_folded(1, 2)
+        num_whole(1, 3)
+        finish(nc.gpsimd, 0)
+        finish(nc.gpsimd, 1)
+        finish(nc.gpsimd, 2)
+        finish(nc.vector, 3)

@@ -1,6 +1,7 @@
 from contextlib import ExitStack
 
 import concourse.mybir as mybir
+from concourse.masks import make_identity
 
 K, L, T, B, N = 1024, 512, 1024, 128, 512
 FLOPS = 2 * N * T * (2 * K + L)
@@ -26,16 +27,22 @@ TILES = N // P
 GROUP = T // B
 GROUPS = HALF // GROUP
 WG_ROW = 4
+PLAIN = (0, 3)
+TURNED = (1, 2)
+DEN_ORDER = PLAIN + TURNED
 
 
 def tile_mix_gated_mean_of_neighbours_kernel(
     tc, xt_words, xt_scales, wv_words, wv_scales, xq, wq_words, wq_scales, wg_words, wg_scales, bw, out
 ):
     nc = tc.nc
+    plain_a, plain_b = PLAIN
+    turned_a, turned_b = TURNED
 
     with ExitStack() as ctx:
         keep = ctx.enter_context(tc.tile_pool(name="keep", bufs=1))
-        psum = ctx.enter_context(tc.psum_pool(name="psum", bufs=8))
+        gate_banks = ctx.enter_context(tc.psum_pool(name="gate_banks", bufs=4))
+        value_banks = ctx.enter_context(tc.psum_pool(name="value_banks", bufs=4))
         ctx.enter_context(tc.manual_schedule())
 
         def sb(name, shape, dtype):
@@ -52,25 +59,29 @@ def tile_mix_gated_mean_of_neighbours_kernel(
         xq_bf = [sb("xq_bf%d" % c, [P, CHUNK * PACK], BF16) for c in range(T // CHUNK)]
         xq_codes = [sb("xq_codes%d" % h, [P, HALF], U32) for h in range(HALVES)]
         xq_plane = [sb("xq_plane%d" % h, [P, HALF], U8) for h in range(HALVES)]
-        bw_all = sb("bw_all", [P, B], F32)
+        bw_col = sb("bw_col", [P, 1], F32)
         warm = sb("warm", [P, 2], F32)
-        gate = {(h, i): sb("gate%d%d" % (h, i), [P, HALF], F32) for h in range(HALVES) for i in range(TILES)}
-        prod = {(h, i): sb("prod%d%d" % (h, i), [P, HALF], F32) for h in range(HALVES) for i in range(TILES)}
-        fold = {(h, i): sb("fold%d%d" % (h, i), [P, GROUPS, 4], F32) for h in range(HALVES) for i in range(TILES)}
-        den = [sb("den%d" % h, [P, TILES, GROUPS], F32) for h in range(HALVES)]
-        den4 = sb("den4", [P, TILES, GROUPS, 4], F32)
-        den2 = sb("den2", [P, TILES * GROUPS, 2], F32)
-        root = sb("root", [P, TILES, B], F32)
-        recip = sb("recip", [P, TILES, B], F32)
-        factor = [sb("factor%d" % u, [P, 2, B], F32) for u in range(2)]
-        num = [sb("num%d" % i, [P, B], F32) for i in range(TILES)]
-        res = [sb("res%d" % i, [P, B], F32) for i in range(TILES)]
+        ident = sb("ident", [P, P], F32)
+        gate = {(h, i): sb("gate%d%d" % (h, i), [P, HALF], F32) for h in range(HALVES) for i in PLAIN}
+        prod = {(h, i): sb("prod%d%d" % (h, i), [P, HALF], F32) for h in range(HALVES) for i in PLAIN}
+        den = {i: sb("den%d" % i, [P, B], F32) for i in PLAIN}
+        gate_by_j = {i: sb("gate_by_j%d" % i, [P, GROUP, B], F32) for i in TURNED}
+        prod_by_j = [sb("prod_by_j%d" % h, [P, len(TURNED), GROUP, GROUPS], F32) for h in range(HALVES)]
+        sum4 = sb("sum4", [P, len(TURNED), 4, B], F32)
+        num = {i: sb("num%d" % i, [P, B], F32) for i in PLAIN}
+        res_t = sb("res_t", [P, len(TURNED) * P], F32)
+        res_turned = sb("res_turned", [P, len(TURNED), B], F32)
+        res = {i: sb("res%d" % i, [P, B], F32) for i in PLAIN}
+        root = sb("root", [P, N], F32)
+        recip = sb("recip", [P, N], F32)
+        factor_t = sb("factor_t", [P, N], F32)
 
-        def load_scales(queue, plane, row, scales, quad):
+        def load_scales(queue, plane, row, scales, quads):
             passes, width = scales.shape[0], scales.shape[2]
-            dst = plane[32 * quad + row : 32 * quad + row + 4, 0 : passes * width].bitcast(I32)
-            src = scales[:, 4 * quad : 4 * quad + 4, :].bitcast(I32)
-            queue.dma_start(out=dst.rearrange("r (z c) -> r z c", z=passes), in_=src.rearrange("z r c -> r z c"))
+            for quad in quads:
+                dst = plane[32 * quad + row : 32 * quad + row + 4, 0 : passes * width].bitcast(I32)
+                src = scales[:, 4 * quad : 4 * quad + 4, :].bitcast(I32)
+                queue.dma_start(out=dst.rearrange("r (z c) -> r z c", z=passes), in_=src.rearrange("z r c -> r z c"))
 
         def load_xt(h):
             src = xt_words.rearrange("z p c r -> p z (c r)")[:, :, PACK * HALF * h : PACK * HALF * (h + 1)]
@@ -80,38 +91,53 @@ def tile_mix_gated_mean_of_neighbours_kernel(
             src = xq[:, CHUNK * c : CHUNK * (c + 1)].rearrange("(p j) t -> p j t", j=PACK)
             nc.sync.dma_start(out=xq_raw[c][:], in_=src)
 
+        def load_wg():
+            nc.sync.dma_start(out=wg[:].bitcast(I32), in_=wg_words.rearrange("z p c r -> p z (c r)").bitcast(I32))
+
+        def load_wv():
+            nc.sync.dma_start(out=wv[:].bitcast(I32), in_=wv_words.rearrange("z p c -> p z c").bitcast(I32))
+
+        def load_wq():
+            nc.sync.dma_start(out=wq[:].bitcast(I32), in_=wq_words[0].bitcast(I32))
+
         nc.vector.memset(plane_x[:].bitcast(I32), 0)
         nc.vector.memset(warm[:, 0:1], 0.0)
-        nc.gpsimd.memset(plane_v[:].bitcast(I32), 0)
-        nc.gpsimd.memset(plane_q[:].bitcast(I32), 0)
+        nc.vector.memset(plane_v[:].bitcast(I32), 0)
+        nc.vector.memset(plane_q[:].bitcast(I32), 0)
         nc.scalar.activation(out=warm[:, 1:2], in_=warm[:, 0:1], func=ACT.Sigmoid)
+        make_identity(nc, ident[:])
 
-        nc.sync.dma_start(out=wg[:].bitcast(I32), in_=wg_words.rearrange("z p c r -> p z (c r)").bitcast(I32))
-        for quad in range(4):
-            load_scales(nc.sync, plane_x, 0, xt_scales, quad)
-        for quad in range(2):
-            load_scales(nc.sync, plane_x, WG_ROW, wg_scales, quad)
+        load_wg()
+        load_scales(nc.sync, plane_x, 0, xt_scales, (0, 1, 2, 3,))
+        load_scales(nc.sync, plane_x, WG_ROW, wg_scales, (0, 1,))
         load_xt(0)
-        for quad in range(2, 4):
-            load_scales(nc.sync, plane_x, WG_ROW, wg_scales, quad)
-        for quad in range(4):
-            load_scales(nc.gpsimd, plane_v, 0, wv_scales, quad)
-        load_xt(1)
+        load_scales(nc.sync, plane_x, WG_ROW, wg_scales, (2, 3,))
         load_xq(0)
+        load_xt(1)
+        load_scales(nc.sync, plane_v, 0, wv_scales, (0, 1, 2,))
         load_xq(1)
-        nc.sync.dma_start(out=wv[:].bitcast(I32), in_=wv_words.rearrange("z p c -> p z c").bitcast(I32))
-        nc.sync.dma_start(out=wq[:].bitcast(I32), in_=wq_words[0].bitcast(I32))
-        for quad in range(4):
-            load_scales(nc.sync, plane_q, 0, wq_scales, quad)
+        load_wv()
+        load_wq()
+        load_scales(nc.sync, plane_v, 0, wv_scales, (3,))
+        load_scales(nc.sync, plane_q, 0, wq_scales, (0, 1, 2, 3,))
         load_xq(2)
         load_xq(3)
-        nc.sync.dma_start(out=bw_all[:], in_=bw[0].partition_broadcast(P))
+        nc.sync.dma_start(out=bw_col[:], in_=bw.rearrange("o b -> b o"))
 
         def xt_plane(h, z):
             return plane_x[:, T * z + HALF * h : T * z + HALF * (h + 1)]
 
+        def groups(h):
+            return slice(GROUPS * h, GROUPS * (h + 1))
+
+        def by_group(t):
+            return t[:].rearrange("p (b j) -> p b j", j=GROUP)
+
+        def by_j(t):
+            return t[:].rearrange("p (b j) -> p j b", j=GROUP)
+
         def gates(h, i):
-            acc = psum.tile([P, HALF], F32, name="acc")
+            acc = gate_banks.tile([P, HALF], F32, name="acc")
             for z in range(PASSES):
                 nc.tensor.matmul_mx(
                     out=acc[:],
@@ -122,12 +148,28 @@ def tile_mix_gated_mean_of_neighbours_kernel(
                     start=(z == 0),
                     stop=(z == PASSES - 1),
                 )
-            nc.scalar.activation(out=gate[h, i][:], in_=acc[:], func=ACT.Sigmoid)
+            if i in PLAIN:
+                nc.scalar.activation(out=gate[h, i][:], in_=acc[:], func=ACT.Sigmoid)
+            else:
+                nc.scalar.activation(out=gate_by_j[i][:, :, groups(h)], in_=by_j(acc), func=ACT.Sigmoid)
+
+        def warm_up(passes):
+            idle = gate_banks.tile([P, HALF], F32, name="acc")
+            for z in range(passes):
+                nc.tensor.matmul_mx(
+                    out=idle[:],
+                    lhsT=wg[:, 0, 0:P].bitcast(FP8X4),
+                    lhsT_scale=plane_x[:, T : T + P],
+                    rhs=wg[:, 1, :].bitcast(FP8X4),
+                    rhs_scale=plane_x[:, T : T + N],
+                    start=True,
+                    stop=True,
+                )
 
         value = {}
 
         def values(h, i):
-            acc = psum.tile([P, HALF], F32, name="acc")
+            acc = value_banks.tile([P, HALF], F32, name="value")
             for z in range(PASSES):
                 nc.tensor.matmul_mx(
                     out=acc[:],
@@ -154,6 +196,14 @@ def tile_mix_gated_mean_of_neighbours_kernel(
             src = xq_raw[c][:].rearrange("p j (c i) -> p c j i", i=4)
             return dst, src
 
+        def cast_on_vector(c):
+            dst, src = cast_views(c)
+            nc.vector.tensor_copy(out=dst, in_=src)
+
+        def cast_on_scalar(c):
+            dst, src = cast_views(c)
+            nc.scalar.copy(out=dst, in_=src)
+
         def quantise(c):
             h, u = divmod(c, HALF // CHUNK)
             cols = slice(CHUNK * u, CHUNK * (u + 1))
@@ -161,111 +211,135 @@ def tile_mix_gated_mean_of_neighbours_kernel(
                 out=xq_codes[h][:, cols].bitcast(FP8X4), scales=xq_plane[h][:, cols], in_=xq_bf[c][:]
             )
 
-        def by_group(t):
-            return t[:].rearrange("p (b j) -> p b j", j=GROUP)
-
         def den_on_vector(h, i):
-            nc.vector.tensor_reduce(out=den[h][:, i, :], in_=by_group(gate[h, i]), axis=AX.X, op=ALU.add)
+            nc.vector.tensor_reduce(out=den[i][:, groups(h)], in_=by_group(gate[h, i]), axis=AX.X, op=ALU.add)
 
-        def fold_halves(dst, t):
-            g = by_group(t)
-            nc.gpsimd.tensor_tensor(out=dst, in0=g[:, :, 0:4], in1=g[:, :, 4:8], op=ALU.add)
+        def den_turn(first, count):
+            den_t = gate_banks.tile([P, HALF], F32, name="acc")
+            for place, i in enumerate(DEN_ORDER[first : first + count]):
+                parts = [den[i][:]] if i in PLAIN else [gate_by_j[i][:, j, :] for j in range(GROUP)]
+                for j, part in enumerate(parts):
+                    nc.tensor.matmul(
+                        den_t[:, P * place : P * (place + 1)],
+                        lhsT=part,
+                        rhs=ident[:],
+                        is_transpose=True,
+                        start=(j == 0),
+                        stop=(j == len(parts) - 1),
+                    )
+            cols = slice(P * first, P * (first + count))
+            nc.scalar.activation(
+                out=root[:, cols], in_=den_t[:, 0 : P * count], func=ACT.Abs_reciprocal_sqrt, bias=0.1
+            )
+            nc.scalar.activation(out=recip[:, cols], in_=root[:, cols], func=ACT.Square)
+            nc.scalar.activation(out=factor_t[:, cols], in_=recip[:, cols], func=ACT.Copy, scale=bw_col[:])
 
         def product(h, i):
-            nc.vector.tensor_tensor(out=prod[h, i][:], in0=value[h, i][:], in1=gate[h, i][:], op=ALU.mult)
+            if i in PLAIN:
+                nc.vector.tensor_tensor(out=prod[h, i][:], in0=value[h, i][:], in1=gate[h, i][:], op=ALU.mult)
+            else:
+                nc.vector.tensor_tensor(
+                    out=prod_by_j[h][:, TURNED.index(i), :, :],
+                    in0=by_j(value[h, i]),
+                    in1=gate_by_j[i][:, :, groups(h)],
+                    op=ALU.mult,
+                )
 
-        def num_cols(h, i):
-            return num[i][:, GROUPS * h : GROUPS * (h + 1)]
+        def num_plain(h, i):
+            nc.vector.tensor_reduce(out=num[i][:, groups(h)], in_=by_group(prod[h, i]), axis=AX.X, op=ALU.add)
 
-        def num_whole(h, i):
-            nc.vector.tensor_reduce(out=num_cols(h, i), in_=by_group(prod[h, i]), axis=AX.X, op=ALU.add)
-
-        def num_fold(h, i):
-            fold_halves(fold[h, i][:], prod[h, i])
-
-        def num_folded(h, i):
-            nc.vector.tensor_reduce(out=num_cols(h, i), in_=fold[h, i][:], axis=AX.X, op=ALU.add)
-
-        def weigh(u):
-            nc.gpsimd.tensor_tensor(
-                out=factor[u][:],
-                in0=recip[:, 2 * u : 2 * u + 2, :],
-                in1=bw_all[:].unsqueeze(1).to_broadcast([P, 2, B]),
-                op=ALU.mult,
+        def halve8(h):
+            nc.vector.tensor_tensor(
+                out=sum4[:, :, :, groups(h)], in0=prod_by_j[h][:, :, 0:4, :], in1=prod_by_j[h][:, :, 4:8, :], op=ALU.add
             )
 
-        def finish(engine, i):
-            engine.tensor_tensor(out=res[i][:], in0=num[i][:], in1=factor[i // 2][:, i % 2, :], op=ALU.mult)
+        banks = {}
+
+        def factors_back():
+            banks["factor"] = gate_banks.tile([P, HALF], F32, name="acc")
+            for place in range(len(PLAIN)):
+                cols = slice(P * place, P * (place + 1))
+                nc.tensor.transpose(banks["factor"][:, cols], factor_t[:, cols], ident[:])
+
+        def num_turn():
+            banks["num"] = gate_banks.tile([P, HALF], F32, name="acc")
+            for place in range(len(TURNED)):
+                for j in range(4):
+                    nc.tensor.matmul(
+                        banks["num"][:, P * place : P * (place + 1)],
+                        lhsT=sum4[:, place, j, :],
+                        rhs=ident[:],
+                        is_transpose=True,
+                        start=(j == 0),
+                        stop=(j == 3),
+                    )
+
+        def weigh_turned():
+            nc.vector.tensor_tensor(out=res_t[:], in0=banks["num"][:, 0 : 2 * P], in1=factor_t[:, 2 * P : N], op=ALU.mult)
+
+        def finish_turned():
+            back = gate_banks.tile([P, HALF], F32, name="acc")
+            for place in range(len(TURNED)):
+                cols = slice(P * place, P * (place + 1))
+                nc.tensor.transpose(back[:, cols], res_t[:, cols], ident[:])
+            nc.scalar.copy(out=res_turned[:].rearrange("p i b -> p (i b)"), in_=back[:, 0 : 2 * P])
+            nc.scalar.dma_start(
+                out=out[P * turned_a : P * (turned_b + 1), :].rearrange("(i p) b -> p i b", p=P), in_=res_turned[:]
+            )
+
+        def finish_plain(i):
+            place = PLAIN.index(i)
+            nc.vector.tensor_tensor(
+                out=res[i][:], in0=banks["factor"][:, P * place : P * (place + 1)], in1=num[i][:], op=ALU.mult
+            )
             nc.sync.dma_start(out=out[P * i : P * (i + 1), :], in_=res[i][:])
 
-        for i in range(TILES):
-            gates(0, i)
-            den_on_vector(0, i)
-        for i in range(TILES):
-            gates(1, i)
-
-        nc.gpsimd.tensor_scalar(
-            out=xq_bf[0][:].rearrange("p (t j) -> p t j", j=PACK),
-            in0=xq_raw[0][:].rearrange("p j t -> p t j"),
-            scalar1=1.0,
-            scalar2=0.0,
-            op0=ALU.mult,
-            op1=ALU.add,
-        )
-        dst, src = cast_views(1)
-        nc.vector.tensor_copy(out=dst, in_=src)
+        gates(0, plain_a)
+        gates(0, plain_b)
+        gates(0, turned_a)
+        gates(0, turned_b)
+        gates(1, plain_a)
+        gates(1, plain_b)
+        gates(1, turned_a)
+        gates(1, turned_b)
+        cast_on_vector(0)
+        den_on_vector(0, plain_a)
         quantise(0)
+        den_on_vector(0, plain_b)
+        cast_on_vector(1)
+        den_on_vector(1, plain_a)
         quantise(1)
-        for c in (2, 3):
-            dst, src = cast_views(c)
-            nc.scalar.copy(out=dst, in_=src)
-
-        for i in range(TILES):
-            fold_halves(den4[:, i, :, :], gate[1, i])
-        quarters = den4[:].rearrange("p i b j -> p (i b) j")
-        nc.gpsimd.tensor_tensor(out=den2[:], in0=quarters[:, :, 0:2], in1=quarters[:, :, 2:4], op=ALU.add)
-        nc.gpsimd.tensor_tensor(
-            out=den[1][:].rearrange("p i b -> p (i b)"), in0=den2[:, :, 0], in1=den2[:, :, 1], op=ALU.add
-        )
-        for h in range(HALVES):
-            nc.scalar.activation(
-                out=root[:, :, GROUPS * h : GROUPS * (h + 1)], in_=den[h][:], func=ACT.Abs_reciprocal_sqrt, bias=0.1
-            )
-        nc.scalar.activation(out=recip[:], in_=root[:], func=ACT.Square)
-
-        values(0, 0)
-        product(0, 0)
-        num_whole(0, 0)
-        values(0, 1)
-        product(0, 1)
-        values(0, 2)
-        product(0, 2)
+        den_on_vector(1, plain_b)
+        cast_on_scalar(2)
+        cast_on_scalar(3)
+        values(0, plain_a)
+        values(0, plain_b)
+        values(0, turned_a)
+        values(0, turned_b)
+        den_turn(0, 4)
+        product(0, plain_a)
+        product(0, plain_b)
+        num_plain(0, plain_a)
+        product(0, turned_a)
         quantise(2)
+        num_plain(0, plain_b)
         quantise(3)
-        num_whole(0, 1)
-        num_whole(0, 2)
-        values(0, 3)
-        product(0, 3)
-        num_fold(0, 3)
-        values(1, 0)
-        product(1, 0)
-        num_fold(1, 0)
-        num_folded(0, 3)
-        weigh(0)
-        values(1, 1)
-        product(1, 1)
-        num_fold(1, 1)
-        num_folded(1, 0)
-        weigh(1)
-        values(1, 2)
-        product(1, 2)
-        num_fold(1, 2)
-        num_folded(1, 1)
-        values(1, 3)
-        product(1, 3)
-        num_folded(1, 2)
-        num_whole(1, 3)
-        finish(nc.gpsimd, 0)
-        finish(nc.gpsimd, 1)
-        finish(nc.gpsimd, 2)
-        finish(nc.vector, 3)
+        product(0, turned_b)
+        halve8(0)
+        values(1, turned_a)
+        values(1, turned_b)
+        values(1, plain_a)
+        values(1, plain_b)
+        factors_back()
+        product(1, turned_a)
+        product(1, turned_b)
+        halve8(1)
+        num_turn()
+        product(1, plain_a)
+        product(1, plain_b)
+        num_plain(1, plain_a)
+        weigh_turned()
+        finish_turned()
+        num_plain(1, plain_b)
+        finish_plain(plain_a)
+        finish_plain(plain_b)

@@ -60,7 +60,6 @@ def tile_mix_gated_mean_of_neighbours_kernel(
         xq_codes = [sb("xq_codes%d" % h, [P, HALF], U32) for h in range(HALVES)]
         xq_plane = [sb("xq_plane%d" % h, [P, HALF], U8) for h in range(HALVES)]
         bw_col = sb("bw_col", [P, 1], F32)
-        warm = sb("warm", [P, 2], F32)
         ident = sb("ident", [P, P], F32)
         gate = {(h, i): sb("gate%d%d" % (h, i), [P, HALF], F32) for h in range(HALVES) for i in PLAIN}
         prod = {(h, i): sb("prod%d%d" % (h, i), [P, HALF], F32) for h in range(HALVES) for i in PLAIN}
@@ -101,10 +100,8 @@ def tile_mix_gated_mean_of_neighbours_kernel(
             nc.sync.dma_start(out=wq[:].bitcast(I32), in_=wq_words[0].bitcast(I32))
 
         nc.vector.memset(plane_x[:].bitcast(I32), 0)
-        nc.vector.memset(warm[:, 0:1], 0.0)
         nc.vector.memset(plane_v[:].bitcast(I32), 0)
         nc.vector.memset(plane_q[:].bitcast(I32), 0)
-        nc.scalar.activation(out=warm[:, 1:2], in_=warm[:, 0:1], func=ACT.Sigmoid)
         make_identity(nc, ident[:])
 
         load_wg()
@@ -294,6 +291,7 @@ def tile_mix_gated_mean_of_neighbours_kernel(
             )
             nc.sync.dma_start(out=out[P * i : P * (i + 1), :], in_=res[i][:])
 
+        warm_up(3)
         gates(0, plain_a)
         gates(0, plain_b)
         gates(0, turned_a)
@@ -316,7 +314,7 @@ def tile_mix_gated_mean_of_neighbours_kernel(
         values(0, plain_b)
         values(0, turned_a)
         values(0, turned_b)
-        den_turn(0, 4)
+        den_turn(0, 3)
         product(0, plain_a)
         product(0, plain_b)
         num_plain(0, plain_a)
@@ -329,6 +327,7 @@ def tile_mix_gated_mean_of_neighbours_kernel(
         values(1, turned_a)
         values(1, turned_b)
         values(1, plain_a)
+        den_turn(3, 1)
         values(1, plain_b)
         factors_back()
         product(1, turned_a)
@@ -336,10 +335,10 @@ def tile_mix_gated_mean_of_neighbours_kernel(
         halve8(1)
         num_turn()
         product(1, plain_a)
-        product(1, plain_b)
         num_plain(1, plain_a)
+        product(1, plain_b)
         weigh_turned()
         finish_turned()
-        num_plain(1, plain_b)
         finish_plain(plain_a)
+        num_plain(1, plain_b)
         finish_plain(plain_b)

from contextlib import ExitStack

import concourse.mybir as mybir
from concourse.masks import make_identity

K, L, T, B, N = 1024, 512, 1024, 128, 512
FLOPS = 2 * N * T * (2 * K + L)

F32 = mybir.dt.float32
BF16 = mybir.dt.bfloat16
I32 = mybir.dt.int32
U32 = mybir.dt.uint32
U8 = mybir.dt.uint8
FP8X4 = mybir.dt.float8_e4m3fn_x4
FP4X4 = mybir.dt.float4_e2m1fn_x4
ACT = mybir.ActivationFunctionType
ALU = mybir.AluOpType
AX = mybir.AxisListType

P = 128
PACK = 4
PASSES = K // (P * PACK)
HALF = 512
HALVES = T // HALF
CHUNK = 256
TILES = N // P
GROUP = T // B
GROUPS = HALF // GROUP
WG_ROW = 4
PLAIN = (0, 3)
TURNED = (1, 2)
DEN_ORDER = PLAIN + TURNED


def tile_mix_gated_mean_of_neighbours_kernel(
    tc, xt_words, xt_scales, wv_words, wv_scales, xq, wq_words, wq_scales, wg_words, wg_scales, bw, out
):
    nc = tc.nc
    plain_a, plain_b = PLAIN
    turned_a, turned_b = TURNED

    with ExitStack() as ctx:
        keep = ctx.enter_context(tc.tile_pool(name="keep", bufs=1))
        gate_banks = ctx.enter_context(tc.psum_pool(name="gate_banks", bufs=4))
        value_banks = ctx.enter_context(tc.psum_pool(name="value_banks", bufs=4))
        ctx.enter_context(tc.manual_schedule())

        def sb(name, shape, dtype):
            return keep.tile(shape, dtype, name=name, align_bytes=64)

        plane_x = sb("plane_x", [P, PASSES * T], U8)
        plane_v = sb("plane_v", [P, PASSES * N], U8)
        plane_q = sb("plane_q", [P, N], U8)
        wg = sb("wg", [P, PASSES, N], U32)
        wv = sb("wv", [P, PASSES, 2 * N], U8)
        wq = sb("wq", [P, 2 * N], U8)
        xt = [sb("xt%d" % h, [P, PASSES, HALF], U32) for h in range(HALVES)]
        xq_raw = [sb("xq_raw%d" % c, [P, PACK, CHUNK], F32) for c in range(T // CHUNK)]
        xq_bf = [sb("xq_bf%d" % c, [P, CHUNK * PACK], BF16) for c in range(T // CHUNK)]
        xq_codes = [sb("xq_codes%d" % h, [P, HALF], U32) for h in range(HALVES)]
        xq_plane = [sb("xq_plane%d" % h, [P, HALF], U8) for h in range(HALVES)]
        bw_col = sb("bw_col", [P, 1], F32)
        ident = sb("ident", [P, P], F32)
        gate = {(h, i): sb("gate%d%d" % (h, i), [P, HALF], F32) for h in range(HALVES) for i in PLAIN}
        prod = {(h, i): sb("prod%d%d" % (h, i), [P, HALF], F32) for h in range(HALVES) for i in PLAIN}
        den = {i: sb("den%d" % i, [P, B], F32) for i in PLAIN}
        gate_by_j = {i: sb("gate_by_j%d" % i, [P, GROUP, B], F32) for i in TURNED}
        prod_by_j = [sb("prod_by_j%d" % h, [P, len(TURNED), GROUP, GROUPS], F32) for h in range(HALVES)]
        sum4 = sb("sum4", [P, len(TURNED), 4, B], F32)
        num = {i: sb("num%d" % i, [P, B], F32) for i in PLAIN}
        res_t = sb("res_t", [P, len(TURNED) * P], F32)
        res_turned = sb("res_turned", [P, len(TURNED), B], F32)
        res = {i: sb("res%d" % i, [P, B], F32) for i in PLAIN}
        root = sb("root", [P, N], F32)
        recip = sb("recip", [P, N], F32)
        factor_t = sb("factor_t", [P, N], F32)

        def load_scales(queue, plane, row, scales, quads):
            passes, width = scales.shape[0], scales.shape[2]
            for quad in quads:
                dst = plane[32 * quad + row : 32 * quad + row + 4, 0 : passes * width].bitcast(I32)
                src = scales[:, 4 * quad : 4 * quad + 4, :].bitcast(I32)
                queue.dma_start(out=dst.rearrange("r (z c) -> r z c", z=passes), in_=src.rearrange("z r c -> r z c"))

        def load_xt(h):
            src = xt_words.rearrange("z p c r -> p z (c r)")[:, :, PACK * HALF * h : PACK * HALF * (h + 1)]
            nc.sync.dma_start(out=xt[h][:].bitcast(I32), in_=src.bitcast(I32))

        def load_xq(c):
            src = xq[:, CHUNK * c : CHUNK * (c + 1)].rearrange("(p j) t -> p j t", j=PACK)
            nc.sync.dma_start(out=xq_raw[c][:], in_=src)

        def load_wg():
            nc.sync.dma_start(out=wg[:].bitcast(I32), in_=wg_words.rearrange("z p c r -> p z (c r)").bitcast(I32))

        def load_wv():
            nc.sync.dma_start(out=wv[:].bitcast(I32), in_=wv_words.rearrange("z p c -> p z c").bitcast(I32))

        def load_wq():
            nc.sync.dma_start(out=wq[:].bitcast(I32), in_=wq_words[0].bitcast(I32))

        nc.vector.memset(plane_x[:].bitcast(I32), 0)
        nc.vector.memset(plane_v[:].bitcast(I32), 0)
        nc.vector.memset(plane_q[:].bitcast(I32), 0)
        make_identity(nc, ident[:])

        load_wg()
        load_scales(nc.sync, plane_x, 0, xt_scales, (0, 1, 2, 3,))
        load_scales(nc.sync, plane_x, WG_ROW, wg_scales, (0, 1,))
        load_xt(0)
        load_scales(nc.sync, plane_x, WG_ROW, wg_scales, (2, 3,))
        load_xq(0)
        load_xt(1)
        load_scales(nc.sync, plane_v, 0, wv_scales, (0, 1, 2,))
        load_xq(1)
        load_wv()
        load_wq()
        load_scales(nc.sync, plane_v, 0, wv_scales, (3,))
        load_scales(nc.sync, plane_q, 0, wq_scales, (0, 1, 2, 3,))
        load_xq(2)
        load_xq(3)
        nc.sync.dma_start(out=bw_col[:], in_=bw.rearrange("o b -> b o"))

        def xt_plane(h, z):
            return plane_x[:, T * z + HALF * h : T * z + HALF * (h + 1)]

        def groups(h):
            return slice(GROUPS * h, GROUPS * (h + 1))

        def by_group(t):
            return t[:].rearrange("p (b j) -> p b j", j=GROUP)

        def by_j(t):
            return t[:].rearrange("p (b j) -> p j b", j=GROUP)

        def gates(h, i):
            acc = gate_banks.tile([P, HALF], F32, name="acc")
            for z in range(PASSES):
                nc.tensor.matmul_mx(
                    out=acc[:],
                    lhsT=wg[:, z, P * i : P * (i + 1)].bitcast(FP8X4),
                    lhsT_scale=plane_x[WG_ROW:P, N * z + P * i : N * z + P * (i + 1)],
                    rhs=xt[h][:, z, :].bitcast(FP8X4),
                    rhs_scale=xt_plane(h, z),
                    start=(z == 0),
                    stop=(z == PASSES - 1),
                )
            if i in PLAIN:
                nc.scalar.activation(out=gate[h, i][:], in_=acc[:], func=ACT.Sigmoid)
            else:
                nc.scalar.activation(out=gate_by_j[i][:, :, groups(h)], in_=by_j(acc), func=ACT.Sigmoid)

        def warm_up(passes):
            idle = gate_banks.tile([P, HALF], F32, name="acc")
            for z in range(passes):
                nc.tensor.matmul_mx(
                    out=idle[:],
                    lhsT=wg[:, 0, 0:P].bitcast(FP8X4),
                    lhsT_scale=plane_x[:, T : T + P],
                    rhs=wg[:, 1, :].bitcast(FP8X4),
                    rhs_scale=plane_x[:, T : T + N],
                    start=True,
                    stop=True,
                )

        value = {}

        def values(h, i):
            acc = value_banks.tile([P, HALF], F32, name="value")
            for z in range(PASSES):
                nc.tensor.matmul_mx(
                    out=acc[:],
                    lhsT=wv[:, z, 2 * P * i : 2 * P * (i + 1)].bitcast(FP4X4),
                    lhsT_scale=plane_v[:, N * z + P * i : N * z + P * (i + 1)],
                    rhs=xt[h][:, z, :].bitcast(FP8X4),
                    rhs_scale=xt_plane(h, z),
                    start=(z == 0),
                    stop=False,
                )
            nc.tensor.matmul_mx(
                out=acc[:],
                lhsT=wq[:, 2 * P * i : 2 * P * (i + 1)].bitcast(FP4X4),
                lhsT_scale=plane_q[:, P * i : P * (i + 1)],
                rhs=xq_codes[h][:].bitcast(FP8X4),
                rhs_scale=xq_plane[h][:],
                start=False,
                stop=True,
            )
            value[h, i] = acc

        def cast_views(c):
            dst = xq_bf[c][:].rearrange("p (c i j) -> p c j i", i=4, j=PACK)
            src = xq_raw[c][:].rearrange("p j (c i) -> p c j i", i=4)
            return dst, src

        def cast_on_vector(c):
            dst, src = cast_views(c)
            nc.vector.tensor_copy(out=dst, in_=src)

        def cast_on_scalar(c):
            dst, src = cast_views(c)
            nc.scalar.copy(out=dst, in_=src)

        def quantise(c):
            h, u = divmod(c, HALF // CHUNK)
            cols = slice(CHUNK * u, CHUNK * (u + 1))
            nc.vector.quantize_mx(
                out=xq_codes[h][:, cols].bitcast(FP8X4), scales=xq_plane[h][:, cols], in_=xq_bf[c][:]
            )

        def den_on_vector(h, i):
            nc.vector.tensor_reduce(out=den[i][:, groups(h)], in_=by_group(gate[h, i]), axis=AX.X, op=ALU.add)

        def den_turn(first, count):
            den_t = gate_banks.tile([P, HALF], F32, name="acc")
            for place, i in enumerate(DEN_ORDER[first : first + count]):
                parts = [den[i][:]] if i in PLAIN else [gate_by_j[i][:, j, :] for j in range(GROUP)]
                for j, part in enumerate(parts):
                    nc.tensor.matmul(
                        den_t[:, P * place : P * (place + 1)],
                        lhsT=part,
                        rhs=ident[:],
                        is_transpose=True,
                        start=(j == 0),
                        stop=(j == len(parts) - 1),
                    )
            cols = slice(P * first, P * (first + count))
            nc.scalar.activation(
                out=root[:, cols], in_=den_t[:, 0 : P * count], func=ACT.Abs_reciprocal_sqrt, bias=0.1
            )
            nc.scalar.activation(out=recip[:, cols], in_=root[:, cols], func=ACT.Square)
            nc.scalar.activation(out=factor_t[:, cols], in_=recip[:, cols], func=ACT.Copy, scale=bw_col[:])

        def product(h, i):
            if i in PLAIN:
                nc.vector.tensor_tensor(out=prod[h, i][:], in0=value[h, i][:], in1=gate[h, i][:], op=ALU.mult)
            else:
                nc.vector.tensor_tensor(
                    out=prod_by_j[h][:, TURNED.index(i), :, :],
                    in0=by_j(value[h, i]),
                    in1=gate_by_j[i][:, :, groups(h)],
                    op=ALU.mult,
                )

        def num_plain(h, i):
            nc.vector.tensor_reduce(out=num[i][:, groups(h)], in_=by_group(prod[h, i]), axis=AX.X, op=ALU.add)

        def halve8(h):
            nc.vector.tensor_tensor(
                out=sum4[:, :, :, groups(h)], in0=prod_by_j[h][:, :, 0:4, :], in1=prod_by_j[h][:, :, 4:8, :], op=ALU.add
            )

        banks = {}

        def factors_back():
            banks["factor"] = gate_banks.tile([P, HALF], F32, name="acc")
            for place in range(len(PLAIN)):
                cols = slice(P * place, P * (place + 1))
                nc.tensor.transpose(banks["factor"][:, cols], factor_t[:, cols], ident[:])

        def num_turn():
            banks["num"] = gate_banks.tile([P, HALF], F32, name="acc")
            for place in range(len(TURNED)):
                for j in range(4):
                    nc.tensor.matmul(
                        banks["num"][:, P * place : P * (place + 1)],
                        lhsT=sum4[:, place, j, :],
                        rhs=ident[:],
                        is_transpose=True,
                        start=(j == 0),
                        stop=(j == 3),
                    )

        def weigh_turned():
            nc.vector.tensor_tensor(out=res_t[:], in0=banks["num"][:, 0 : 2 * P], in1=factor_t[:, 2 * P : N], op=ALU.mult)

        def finish_turned():
            back = gate_banks.tile([P, HALF], F32, name="acc")
            for place in range(len(TURNED)):
                cols = slice(P * place, P * (place + 1))
                nc.tensor.transpose(back[:, cols], res_t[:, cols], ident[:])
            nc.scalar.copy(out=res_turned[:].rearrange("p i b -> p (i b)"), in_=back[:, 0 : 2 * P])
            nc.scalar.dma_start(
                out=out[P * turned_a : P * (turned_b + 1), :].rearrange("(i p) b -> p i b", p=P), in_=res_turned[:]
            )

        def finish_plain(i):
            place = PLAIN.index(i)
            nc.vector.tensor_tensor(
                out=res[i][:], in0=banks["factor"][:, P * place : P * (place + 1)], in1=num[i][:], op=ALU.mult
            )
            nc.sync.dma_start(out=out[P * i : P * (i + 1), :], in_=res[i][:])

        warm_up(3)
        gates(0, plain_a)
        gates(0, plain_b)
        gates(0, turned_a)
        gates(0, turned_b)
        gates(1, plain_a)
        gates(1, plain_b)
        gates(1, turned_a)
        gates(1, turned_b)
        cast_on_vector(0)
        den_on_vector(0, plain_a)
        quantise(0)
        den_on_vector(0, plain_b)
        cast_on_vector(1)
        den_on_vector(1, plain_a)
        quantise(1)
        den_on_vector(1, plain_b)
        cast_on_scalar(2)
        cast_on_scalar(3)
        values(0, plain_a)
        values(0, plain_b)
        values(0, turned_a)
        values(0, turned_b)
        den_turn(0, 3)
        product(0, plain_a)
        product(0, plain_b)
        num_plain(0, plain_a)
        product(0, turned_a)
        quantise(2)
        num_plain(0, plain_b)
        quantise(3)
        product(0, turned_b)
        halve8(0)
        values(1, turned_a)
        values(1, turned_b)
        values(1, plain_a)
        den_turn(3, 1)
        values(1, plain_b)
        factors_back()
        product(1, turned_a)
        product(1, turned_b)
        halve8(1)
        num_turn()
        product(1, plain_a)
        num_plain(1, plain_a)
        product(1, plain_b)
        weigh_turned()
        finish_turned()
        finish_plain(plain_a)
        num_plain(1, plain_b)
        finish_plain(plain_b)
